import numpy as np
import ml_dtypes


def mxq(x, axis, fmt="e4m3"):
    dtype, down = {"e4m3": (ml_dtypes.float8_e4m3fn, 7), "e5m2": (ml_dtypes.float8_e5m2, 14)}[fmt]
    v = np.moveaxis(np.asarray(x, np.float32).astype(ml_dtypes.bfloat16).astype(np.float64), axis, -1)
    blocks = v.reshape(v.shape[:-1] + (-1, 32))
    amax = np.abs(blocks).max(-1, keepdims=True)
    byte = np.maximum(np.where(amax > 0, np.frexp(amax)[1] - 1 + 127, 0) - down, 1)
    scale = np.exp2(byte - 127.0)
    codes = (blocks / scale).astype(np.float32).astype(dtype).astype(np.float64)
    return np.moveaxis((codes * scale).reshape(v.shape), -1, axis)


WIDE = False


def mx_kscale(k):
    if not WIDE:
        return np.ones(k)
    levels = np.array([10, -10, 5, -5, 0])
    if k % 512:
        return np.exp2(np.random.permutation(np.resize(levels, k // 32))).repeat(32)
    a = np.empty((k // 512, 16))
    for p in range(k // 512):
        a[p, :8] = np.random.permutation(np.resize(levels, 8))
        for g in range(8):
            far = levels[np.abs(levels - a[p, g]) >= 10]
            a[p, g + 8] = far[np.random.randint(len(far))]
    return np.exp2(a.ravel()).repeat(32)


def f64(x):
    return np.asarray(x).astype(np.float64)


def striped(idx):
    return np.tile(idx.reshape(-1, 16).T, (8, 1)).astype(np.uint16)


def unstriped(offs):
    return offs[:16].T.reshape(-1).astype(np.int64)


def sigmoid(v):
    return 1.0 / (1.0 + np.exp(-np.maximum(v, -700.0)))


def d_sigmoid(v):
    s = 1.0 / (1.0 + np.exp(-np.maximum(v, -700.0)))
    return s * (1.0 - s)


K, T, E, C, H, N = 768, 1024, 4, 256, 512, 512


def by_expert(wq, xq):
    return np.concatenate([wq[e].T @ xq[:, e * C:(e + 1) * C] for e in range(E)], axis=1)


def setup_inputs():
    n = np.random.standard_normal
    s = mx_kscale(N)[:, None]
    u = mx_kscale(H)
    return {
        "dyT": (n((N, T)) * s).astype(np.float32),
        "a1": n((H, E * C)).astype(np.float32),
        "a3": n((H, E * C)).astype(np.float32),
        "w2": (n((E, N, H)) / np.sqrt(N) / s[None] * u[None, None, :]).astype(np.float32),
        "w1": (n((E, H, K)) / np.sqrt(H) / u[None, :, None]).astype(np.float32),
        "w3": (n((E, H, K)) / np.sqrt(H) / u[None, :, None]).astype(np.float32),
        "gate": np.tile(np.random.uniform(0.2, 1.0, E * C), (N, 1)).astype(np.float32),
        "offs": striped(np.random.permutation(T)[:E * C]),
    }


def reference(dyT, a1, a3, w2, w1, w3, gate, offs):
    idx = unstriped(offs)
    gq = mxq(f64(gate) * f64(dyT)[:, idx], 0, "e4m3")
    dh = by_expert(mxq(f64(w2), 1, "e4m3"), gq)
    da1 = dh * f64(a3) * d_sigmoid(f64(a1))
    da3 = dh * sigmoid(f64(a1))
    dx = by_expert(mxq(f64(w1), 1, "e4m3"), mxq(da1, 0, "e4m3")) + by_expert(mxq(f64(w3), 1, "e4m3"), mxq(da3, 0, "e4m3"))
    out = np.zeros((K, T))
    out[:, idx] = dx
    return out

@@ -1,0 +1,187 @@
+from contextlib import ExitStack
+
+import concourse.mybir as mybir
+
+K, T, E, C, H, N = 768, 1024, 4, 256, 512, 512
+FLOPS = 2 * T * (N * H + 2 * H * K)
+
+F32 = mybir.dt.float32
+BF16 = mybir.dt.bfloat16
+U32 = mybir.dt.uint32
+U16 = mybir.dt.uint16
+U8 = mybir.dt.uint8
+FP8X4 = mybir.dt.float8_e4m3fn_x4
+
+P = 128
+R = 4
+SIGMOID = mybir.ActivationFunctionType.Sigmoid
+MULT = mybir.AluOpType.mult
+KC = 256
+CHUNKS = K // KC
+ADD = mybir.AluOpType.add
+PLACE = {(0, 0, 0): "G", (0, 1, 0): "V"}
+A_ON_VECTOR = [(0, 1)]
+
+
+def tile_moe_bdx_glu_sigmoid_kernel(tc, dyT, a1, a3, w2, w1, w3, gate, offs, out):
+    nc = tc.nc
+    with ExitStack() as ctx:
+        keep = ctx.enter_context(tc.tile_pool(name="keep", bufs=1))
+        pool = ctx.enter_context(tc.tile_pool(name="pool", bufs=2))
+        psum = ctx.enter_context(tc.psum_pool(name="psum", bufs=2))
+
+        offsets = keep.tile([P, T // 16], U16, name="offsets")
+        gates = keep.tile([P, T], F32, name="gates")
+        warm = keep.tile([P, 8], F32, name="warm")
+        warm_out = keep.tile([P, 8], F32, name="warm_out")
+        windows = [keep.tile([P, T], F32, name="window%d" % b) for b in range(K // P)]
+
+        nc.vector.memset(warm[:], 0.0)
+        nc.scalar.activation(warm_out[:], warm[:], SIGMOID)
+
+        dy_view = dyT.rearrange("(p r) c -> p r c", r=R)
+        a1_view = a1.rearrange("(p r) c -> p r c", r=R)
+        a3_view = a3.rearrange("(p r) c -> p r c", r=R)
+
+        def offs_of(e):
+            return offsets[:, e * (C // 16) : (e + 1) * (C // 16)]
+
+        def load_a(view, e):
+            t = pool.tile([P, R, C], F32, name="x4", bufs=8)
+            nc.sync.dma_start(out=t[:], in_=view[:, :, e * C : (e + 1) * C])
+            return t
+
+        def load_w2(e):
+            t = pool.tile([P, R, H], F32, name="w2raw", bufs=2)
+            nc.sync.dma_start(out=t[:], in_=w2[e].rearrange("(p r) c -> p r c", r=R))
+            return t
+
+        def load_w13(e, split):
+            ts = []
+            for i in range(2):
+                t = pool.tile([P, R, K], F32, name="w13raw", bufs=4)
+                ts.append(t)
+            step = KC if split else K
+            for c in range(0, K, step):
+                for t, w in zip(ts, (w1, w3)):
+                    nc.sync.dma_start(out=t[:, :, c : c + step], in_=w[e].rearrange("(p r) c -> p r c", r=R)[:, :, c : c + step])
+            return ts
+
+        def interleave(place, dst, src):
+            if place == "G":
+                nc.gpsimd.tensor_scalar(dst, src.rearrange("p r c -> p c r"), 1.0, 0.0, MULT, ADD)
+            else:
+                copy = nc.vector.tensor_copy if place == "V" else nc.scalar.copy
+                copy(dst.rearrange("p (c i) r -> p c r i", i=4), src.rearrange("p r (c i) -> p c r i", i=4))
+
+        def gather(e):
+            t = pool.tile([P, R, C], F32, name="g32", bufs=4)
+            for r in range(R):
+                nc.vector.tensor_tensor(t[:, r, :], dy[r][:].indirect(offs_of(e)), gates[:, e * C : (e + 1) * C], MULT)
+            return t
+
+        def quantize(dst_name, src, words, bufs):
+            codes = pool.tile([P, words], U32, name=dst_name, bufs=bufs, align_bytes=64)
+            scales = pool.tile([P, words], U8, name=dst_name + "_s", bufs=bufs, align_bytes=64)
+            nc.vector.quantize_mx(out=codes[:].bitcast(FP8X4), scales=scales[:], in_=src[:].rearrange("p c r -> p (c r)"))
+            return codes, scales
+
+        def mm(bank, lhs, l0, rhs, r0, n, start, stop):
+            nc.tensor.matmul_mx(
+                out=bank,
+                lhsT=lhs[0][:, l0 : l0 + P].bitcast(FP8X4),
+                lhsT_scale=lhs[1][:, l0 : l0 + P],
+                rhs=rhs[0][:, r0 : r0 + n].bitcast(FP8X4),
+                rhs_scale=rhs[1][:, r0 : r0 + n],
+                start=start,
+                stop=stop,
+            )
+
+        def chain(e, g32, a1t, a3t, w2raw, w13raw):
+            gbf = pool.tile([P, C, R], BF16, name="gbf", bufs=2, align_bytes=64)
+            interleave("S", gbf[:], g32[:])
+            w2bf = pool.tile([P, H, R], BF16, name="wbf", bufs=3, align_bytes=64)
+            copy = nc.vector.tensor_copy if PLACE.get((e, 0, 2)) == "V" else nc.scalar.copy
+            copy(w2bf[:].rearrange("p (r m) j -> p m j r", r=R), w2raw[:].rearrange("p j (m r) -> p m j r", r=R))
+            s = pool.tile([P, R, C], F32, name="s", bufs=2)
+            u = pool.tile([P, R, C], F32, name="u", bufs=1)
+            q = pool.tile([P, R, C], F32, name="q", bufs=2)
+            nc.scalar.activation(s[:], a1t[:], SIGMOID)
+            nc.scalar.activation(u[:], a1t[:], SIGMOID, scale=-1.0)
+            nc.gpsimd.tensor_tensor(q[:], a3t[:], u[:], MULT)
+
+            gq = quantize("gq", gbf, C, 2)
+            w2q = quantize("wq", w2bf, H, 8)
+
+            da1 = pool.tile([P, C, R], BF16, name="da1", bufs=2, align_bytes=64)
+            da3 = pool.tile([P, C, R], BF16, name="da3", bufs=2, align_bytes=64)
+            half = C // 2
+            for h in range(2):
+                bank = psum.tile([P, R, half], F32, name="dh", bufs=3)
+                for r in range(R):
+                    mm(bank[:, r, :], w2q, r * P, gq, h * half, half, True, True)
+                cols = slice(h * half, (h + 1) * half)
+                d = pool.tile([P, R, half], F32, name="d", bufs=3)
+                if (e, h) in A_ON_VECTOR:
+                    nc.vector.tensor_tensor(d[:], bank[:], s[:, :, cols], MULT)
+                else:
+                    d0 = pool.tile([P, R, half], F32, name="d0", bufs=2)
+                    nc.scalar.copy(d0[:], bank[:])
+                    nc.gpsimd.tensor_tensor(d[:], d0[:], s[:, :, cols], MULT)
+                interleave("S", da3[:, cols, :], d[:])
+                nc.gpsimd.tensor_tensor(da1[:, cols, :], d[:].rearrange("p r c -> p c r"), q[:, :, cols].rearrange("p r c -> p c r"), MULT)
+            da3q = quantize("da3q", da3, C, 2)
+            da1q = quantize("da1q", da1, C, 2)
+
+            results = []
+            for c in range(CHUNKS):
+                wbf = pool.tile([P, 2 * KC, R], BF16, name="wbf", bufs=3, align_bytes=64)
+                for i in range(2):
+                    dst = wbf[:, i * KC : (i + 1) * KC, :]
+                    src = w13raw[i][:, :, c * KC : (c + 1) * KC]
+                    interleave(PLACE.get((e, c, i), "S"), dst, src)
+                wq = quantize("wq", wbf, 2 * KC, 8)
+                bank = psum.tile([P, 2, C], F32, name="dx", bufs=4)
+                for b in range(2):
+                    mm(bank[:, b, :], wq, KC + b * P, da3q, 0, C, True, False)
+                    mm(bank[:, b, :], wq, b * P, da1q, 0, C, False, True)
+                dx = pool.tile([P, 2, C], F32, name="dxs", bufs=6)
+                nc.scalar.copy(dx[:], bank[:])
+                results.append(dx)
+            return results
+
+        def scatter(e, results):
+            for b in range(K // P):
+                nc.vector.tensor_copy(windows[b][:].indirect(offs_of(e)), results[b // 2][:, b % 2, :])
+                if e == E - 1:
+                    nc.sync.dma_start(out=out[b * P : (b + 1) * P, :], in_=windows[b][:])
+
+        nc.sync.dma_start(offsets[:], offs)
+        nc.sync.dma_start(out=gates[:, 0:C], in_=gate[0:P, 0:C])
+        dy = []
+        for r in range(R):
+            t = pool.tile([P, T], F32, name="x4", bufs=8)
+            dy.append(t)
+            nc.sync.dma_start(out=t[:], in_=dy_view[:, r, :])
+            if r == 1:
+                nc.sync.dma_start(out=gates[:, C:T], in_=gate[0:P, C:T])
+
+        def load(e):
+            w2raw = load_w2(e)
+            a1t = load_a(a1_view, e)
+            a3t = load_a(a3_view, e)
+            w = load_w13(e, e == 0)
+            return a1t, a3t, w2raw, w
+
+        loaded = {0: load(0)}
+        loaded[1] = load(1)
+        g = {0: gather(0)}
+        results = {0: chain(0, g[0], *loaded[0])}
+        for e in range(1, E):
+            g[e] = gather(e)
+        for e in range(1, E):
+            if e + 1 < E:
+                loaded[e + 1] = load(e + 1)
+            results[e] = chain(e, g[e], *loaded[e])
+            scatter(e - 1, results[e - 1])
+        scatter(E - 1, results[E - 1])

@@ -16,11 +16,13 @@ P = 128
 R = 4
 SIGMOID = mybir.ActivationFunctionType.Sigmoid
 MULT = mybir.AluOpType.mult
+ADD = mybir.AluOpType.add
 KC = 256
 CHUNKS = K // KC
-ADD = mybir.AluOpType.add
-PLACE = {(0, 0, 0): "G", (0, 1, 0): "V"}
-A_ON_VECTOR = [(0, 1)]
+W_PLACE = {"0.0.0": "V", "0.0.1": "V", "0.1.1": "V"}
+A_PLACE = {}
+A_DEF = "VV"
+B = {"x4": 8, "g32": 4, "gbf": 3, "w2raw": 2, "raw": 4, "wbf": 4, "gq": 2, "wq": 8, "s": 2, "u": 1, "q": 2, "da": 2, "d": 3, "d0": 2, "dxs": 6, "dh": 3, "dx": 4}
 
 
 def tile_moe_bdx_glu_sigmoid_kernel(tc, dyT, a1, a3, w2, w1, w3, gate, offs, out):
@@ -40,32 +42,28 @@ def tile_moe_bdx_glu_sigmoid_kernel(tc, dyT, a1, a3, w2, w1, w3, gate, offs, out
         nc.scalar.activation(warm_out[:], warm[:], SIGMOID)
 
         dy_view = dyT.rearrange("(p r) c -> p r c", r=R)
-        a1_view = a1.rearrange("(p r) c -> p r c", r=R)
-        a3_view = a3.rearrange("(p r) c -> p r c", r=R)
+        st = [{} for e in range(E)]
 
         def offs_of(e):
             return offsets[:, e * (C // 16) : (e + 1) * (C // 16)]
 
-        def load_a(view, e):
-            t = pool.tile([P, R, C], F32, name="x4", bufs=8)
-            nc.sync.dma_start(out=t[:], in_=view[:, :, e * C : (e + 1) * C])
-            return t
-
-        def load_w2(e):
-            t = pool.tile([P, R, H], F32, name="w2raw", bufs=2)
+        def load_a(e):
+            t = pool.tile([P, R, H], F32, name="w2raw", bufs=B["w2raw"])
             nc.sync.dma_start(out=t[:], in_=w2[e].rearrange("(p r) c -> p r c", r=R))
-            return t
+            st[e]["w2"] = t
+            for key, src in (("a1", a1), ("a3", a3)):
+                t = pool.tile([P, R, C], F32, name="x4", bufs=B["x4"])
+                nc.sync.dma_start(out=t[:], in_=src.rearrange("(p r) c -> p r c", r=R)[:, :, e * C : (e + 1) * C])
+                st[e][key] = t
 
-        def load_w13(e, split):
-            ts = []
-            for i in range(2):
-                t = pool.tile([P, R, K], F32, name="w13raw", bufs=4)
-                ts.append(t)
+        def load_w(e, split=False):
+            for key in ("w1", "w3"):
+                t = pool.tile([P, R, K], F32, name="w13raw", bufs=B["raw"])
+                st[e][key] = t
             step = KC if split else K
             for c in range(0, K, step):
-                for t, w in zip(ts, (w1, w3)):
-                    nc.sync.dma_start(out=t[:, :, c : c + step], in_=w[e].rearrange("(p r) c -> p r c", r=R)[:, :, c : c + step])
-            return ts
+                for key, w in (("w1", w1), ("w3", w3)):
+                    nc.sync.dma_start(out=st[e][key][:, :, c : c + step], in_=w[e].rearrange("(p r) c -> p r c", r=R)[:, :, c : c + step])
 
         def interleave(place, dst, src):
             if place == "G":
@@ -75,14 +73,14 @@ def tile_moe_bdx_glu_sigmoid_kernel(tc, dyT, a1, a3, w2, w1, w3, gate, offs, out
                 copy(dst.rearrange("p (c i) r -> p c r i", i=4), src.rearrange("p r (c i) -> p c r i", i=4))
 
         def gather(e):
-            t = pool.tile([P, R, C], F32, name="g32", bufs=4)
+            t = pool.tile([P, R, C], F32, name="g32", bufs=B["g32"])
             for r in range(R):
                 nc.vector.tensor_tensor(t[:, r, :], dy[r][:].indirect(offs_of(e)), gates[:, e * C : (e + 1) * C], MULT)
-            return t
+            st[e]["g"] = t
 
-        def quantize(dst_name, src, words, bufs):
-            codes = pool.tile([P, words], U32, name=dst_name, bufs=bufs, align_bytes=64)
-            scales = pool.tile([P, words], U8, name=dst_name + "_s", bufs=bufs, align_bytes=64)
+        def quantize(name, src, words, bufs):
+            codes = pool.tile([P, words], U32, name=name, bufs=bufs, align_bytes=64)
+            scales = pool.tile([P, words], U8, name=name + "_s", bufs=bufs, align_bytes=64)
             nc.vector.quantize_mx(out=codes[:].bitcast(FP8X4), scales=scales[:], in_=src[:].rearrange("p c r -> p (c r)"))
             return codes, scales
 
@@ -97,62 +95,78 @@ def tile_moe_bdx_glu_sigmoid_kernel(tc, dyT, a1, a3, w2, w1, w3, gate, offs, out
                 stop=stop,
             )
 
-        def chain(e, g32, a1t, a3t, w2raw, w13raw):
-            gbf = pool.tile([P, C, R], BF16, name="gbf", bufs=2, align_bytes=64)
-            interleave("S", gbf[:], g32[:])
-            w2bf = pool.tile([P, H, R], BF16, name="wbf", bufs=3, align_bytes=64)
-            copy = nc.vector.tensor_copy if PLACE.get((e, 0, 2)) == "V" else nc.scalar.copy
-            copy(w2bf[:].rearrange("p (r m) j -> p m j r", r=R), w2raw[:].rearrange("p j (m r) -> p m j r", r=R))
-            s = pool.tile([P, R, C], F32, name="s", bufs=2)
-            u = pool.tile([P, R, C], F32, name="u", bufs=1)
-            q = pool.tile([P, R, C], F32, name="q", bufs=2)
-            nc.scalar.activation(s[:], a1t[:], SIGMOID)
-            nc.scalar.activation(u[:], a1t[:], SIGMOID, scale=-1.0)
-            nc.gpsimd.tensor_tensor(q[:], a3t[:], u[:], MULT)
-
-            gq = quantize("gq", gbf, C, 2)
-            w2q = quantize("wq", w2bf, H, 8)
-
-            da1 = pool.tile([P, C, R], BF16, name="da1", bufs=2, align_bytes=64)
-            da3 = pool.tile([P, C, R], BF16, name="da3", bufs=2, align_bytes=64)
+        def front(e):
+            d = st[e]
+            gbf = pool.tile([P, C, R], BF16, name="gbf", bufs=B["gbf"], align_bytes=64)
+            interleave("S", gbf[:], d["g"][:])
+            w2bf = pool.tile([P, H, R], BF16, name="wbf", bufs=B["wbf"], align_bytes=64)
+            place = W_PLACE.get("%d.w2" % e, "S")
+            out_view = w2bf[:].rearrange("p (r m) j -> p m j r", r=R)
+            in_view = d["w2"][:].rearrange("p j (m r) -> p m j r", r=R)
+            if place == "G":
+                nc.gpsimd.tensor_scalar(out_view, in_view, 1.0, 0.0, MULT, ADD)
+            elif place == "V":
+                nc.vector.tensor_copy(out_view, in_view)
+            else:
+                nc.scalar.copy(out_view, in_view)
+            s = pool.tile([P, R, C], F32, name="s", bufs=B["s"])
+            u = pool.tile([P, R, C], F32, name="u", bufs=B["u"])
+            q = pool.tile([P, R, C], F32, name="q", bufs=B["q"])
+            nc.scalar.activation(s[:], d["a1"][:], SIGMOID)
+            nc.scalar.activation(u[:], d["a1"][:], SIGMOID, scale=-1.0)
+            modes = [A_PLACE.get("%d.%d" % (e, h), A_DEF) for h in range(2)]
+            nc.gpsimd.tensor_tensor(q[:], d["a3"][:], u[:], MULT)
+            if "VV" in modes:
+                cq = pool.tile([P, R, C], F32, name="cq", bufs=B["q"])
+                nc.gpsimd.tensor_tensor(cq[:], q[:], s[:], MULT)
+            gq = quantize("gq", gbf, C, B["gq"])
+            w2q = quantize("wq", w2bf, H, B["wq"])
+            da1 = pool.tile([P, C, R], BF16, name="da1", bufs=B["da"], align_bytes=64)
+            da3 = pool.tile([P, C, R], BF16, name="da3", bufs=B["da"], align_bytes=64)
             half = C // 2
             for h in range(2):
-                bank = psum.tile([P, R, half], F32, name="dh", bufs=3)
+                bank = psum.tile([P, R, half], F32, name="dh", bufs=B["dh"])
                 for r in range(R):
                     mm(bank[:, r, :], w2q, r * P, gq, h * half, half, True, True)
                 cols = slice(h * half, (h + 1) * half)
-                d = pool.tile([P, R, half], F32, name="d", bufs=3)
-                if (e, h) in A_ON_VECTOR:
-                    nc.vector.tensor_tensor(d[:], bank[:], s[:, :, cols], MULT)
+                if modes[h] == "VV":
+                    turned = bank[:].rearrange("p r c -> p c r")
+                    nc.vector.tensor_tensor(da3[:, cols, :], turned, s[:, :, cols].rearrange("p r c -> p c r"), MULT)
+                    nc.vector.tensor_tensor(da1[:, cols, :], turned, cq[:, :, cols].rearrange("p r c -> p c r"), MULT)
+                    continue
+                t = pool.tile([P, R, half], F32, name="d", bufs=B["d"])
+                if modes[h] == "V":
+                    nc.vector.tensor_tensor(t[:], bank[:], s[:, :, cols], MULT)
                 else:
-                    d0 = pool.tile([P, R, half], F32, name="d0", bufs=2)
+                    d0 = pool.tile([P, R, half], F32, name="d0", bufs=B["d0"])
                     nc.scalar.copy(d0[:], bank[:])
-                    nc.gpsimd.tensor_tensor(d[:], d0[:], s[:, :, cols], MULT)
-                interleave("S", da3[:, cols, :], d[:])
-                nc.gpsimd.tensor_tensor(da1[:, cols, :], d[:].rearrange("p r c -> p c r"), q[:, :, cols].rearrange("p r c -> p c r"), MULT)
-            da3q = quantize("da3q", da3, C, 2)
-            da1q = quantize("da1q", da1, C, 2)
+                    nc.gpsimd.tensor_tensor(t[:], d0[:], s[:, :, cols], MULT)
+                interleave("S", da3[:, cols, :], t[:])
+                nc.gpsimd.tensor_tensor(da1[:, cols, :], t[:].rearrange("p r c -> p c r"), q[:, :, cols].rearrange("p r c -> p c r"), MULT)
+            d["da3q"] = quantize("da3q", da3, C, 2)
+            d["da1q"] = quantize("da1q", da1, C, 2)
 
-            results = []
+        def wall(e):
+            d = st[e]
+            d["dx"] = []
             for c in range(CHUNKS):
-                wbf = pool.tile([P, 2 * KC, R], BF16, name="wbf", bufs=3, align_bytes=64)
-                for i in range(2):
+                wbf = pool.tile([P, 2 * KC, R], BF16, name="wbf", bufs=B["wbf"], align_bytes=64)
+                for i, key in enumerate(("w1", "w3")):
                     dst = wbf[:, i * KC : (i + 1) * KC, :]
-                    src = w13raw[i][:, :, c * KC : (c + 1) * KC]
-                    interleave(PLACE.get((e, c, i), "S"), dst, src)
-                wq = quantize("wq", wbf, 2 * KC, 8)
-                bank = psum.tile([P, 2, C], F32, name="dx", bufs=4)
+                    src = d[key][:, :, c * KC : (c + 1) * KC]
+                    interleave(W_PLACE.get("%d.%d.%d" % (e, c, i), "S"), dst, src)
+                wq = quantize("wq", wbf, 2 * KC, B["wq"])
+                bank = psum.tile([P, 2, C], F32, name="dx", bufs=B["dx"])
                 for b in range(2):
-                    mm(bank[:, b, :], wq, KC + b * P, da3q, 0, C, True, False)
-                    mm(bank[:, b, :], wq, b * P, da1q, 0, C, False, True)
-                dx = pool.tile([P, 2, C], F32, name="dxs", bufs=6)
+                    mm(bank[:, b, :], wq, KC + b * P, d["da3q"], 0, C, True, False)
+                    mm(bank[:, b, :], wq, b * P, d["da1q"], 0, C, False, True)
+                dx = pool.tile([P, 2, C], F32, name="dxs", bufs=B["dxs"])
                 nc.scalar.copy(dx[:], bank[:])
-                results.append(dx)
-            return results
+                d["dx"].append(dx)
 
-        def scatter(e, results):
+        def scatter(e):
             for b in range(K // P):
-                nc.vector.tensor_copy(windows[b][:].indirect(offs_of(e)), results[b // 2][:, b % 2, :])
+                nc.vector.tensor_copy(windows[b][:].indirect(offs_of(e)), st[e]["dx"][b // 2][:, b % 2, :])
                 if e == E - 1:
                     nc.sync.dma_start(out=out[b * P : (b + 1) * P, :], in_=windows[b][:])
 
@@ -160,28 +174,33 @@ def tile_moe_bdx_glu_sigmoid_kernel(tc, dyT, a1, a3, w2, w1, w3, gate, offs, out
         nc.sync.dma_start(out=gates[:, 0:C], in_=gate[0:P, 0:C])
         dy = []
         for r in range(R):
-            t = pool.tile([P, T], F32, name="x4", bufs=8)
+            t = pool.tile([P, T], F32, name="x4", bufs=B["x4"])
             dy.append(t)
             nc.sync.dma_start(out=t[:], in_=dy_view[:, r, :])
             if r == 1:
                 nc.sync.dma_start(out=gates[:, C:T], in_=gate[0:P, C:T])
 
-        def load(e):
-            w2raw = load_w2(e)
-            a1t = load_a(a1_view, e)
-            a3t = load_a(a3_view, e)
-            w = load_w13(e, e == 0)
-            return a1t, a3t, w2raw, w
-
-        loaded = {0: load(0)}
-        loaded[1] = load(1)
-        g = {0: gather(0)}
-        results = {0: chain(0, g[0], *loaded[0])}
-        for e in range(1, E):
-            g[e] = gather(e)
-        for e in range(1, E):
-            if e + 1 < E:
-                loaded[e + 1] = load(e + 1)
-            results[e] = chain(e, g[e], *loaded[e])
-            scatter(e - 1, results[e - 1])
-        scatter(E - 1, results[E - 1])
+        load_a(0)
+        load_w(0, True)
+        load_a(1)
+        gather(0)
+        front(0)
+        gather(1)
+        gather(2)
+        gather(3)
+        wall(0)
+        load_w(1)
+        front(1)
+        load_a(2)
+        wall(1)
+        scatter(0)
+        load_w(2)
+        front(2)
+        load_a(3)
+        wall(2)
+        scatter(1)
+        load_w(3)
+        front(3)
+        wall(3)
+        scatter(2)
+        scatter(3)

@@ -16,13 +16,14 @@ P = 128
 R = 4
 SIGMOID = mybir.ActivationFunctionType.Sigmoid
 MULT = mybir.AluOpType.mult
+SUB = mybir.AluOpType.subtract
 ADD = mybir.AluOpType.add
 KC = 256
 CHUNKS = K // KC
-W_PLACE = {"0.0.0": "V", "0.0.1": "V", "0.1.1": "V"}
+W_PLACE = {"0.0.0": "V"}
 A_PLACE = {}
-A_DEF = "VV"
-B = {"x4": 8, "g32": 4, "gbf": 3, "w2raw": 2, "raw": 4, "wbf": 4, "gq": 2, "wq": 8, "s": 2, "u": 1, "q": 2, "da": 2, "d": 3, "d0": 2, "dxs": 6, "dh": 3, "dx": 4}
+A_DEF = "VS"
+B = {"x4": 8, "g32": 4, "gbf": 3, "w2raw": 2, "raw": 4, "wbf": 4, "gq": 2, "wq": 8, "s": 2, "u": 1, "q": 2, "da": 2, "d": 4, "d0": 2, "dxs": 6, "dh": 3, "dx": 4}
 
 
 def tile_moe_bdx_glu_sigmoid_kernel(tc, dyT, a1, a3, w2, w1, w3, gate, offs, out):
@@ -109,40 +110,27 @@ def tile_moe_bdx_glu_sigmoid_kernel(tc, dyT, a1, a3, w2, w1, w3, gate, offs, out
                 nc.vector.tensor_copy(out_view, in_view)
             else:
                 nc.scalar.copy(out_view, in_view)
-            s = pool.tile([P, R, C], F32, name="s", bufs=B["s"])
-            u = pool.tile([P, R, C], F32, name="u", bufs=B["u"])
-            q = pool.tile([P, R, C], F32, name="q", bufs=B["q"])
-            nc.scalar.activation(s[:], d["a1"][:], SIGMOID)
-            nc.scalar.activation(u[:], d["a1"][:], SIGMOID, scale=-1.0)
-            modes = [A_PLACE.get("%d.%d" % (e, h), A_DEF) for h in range(2)]
-            nc.gpsimd.tensor_tensor(q[:], d["a3"][:], u[:], MULT)
-            if "VV" in modes:
-                cq = pool.tile([P, R, C], F32, name="cq", bufs=B["q"])
-                nc.gpsimd.tensor_tensor(cq[:], q[:], s[:], MULT)
+            s = pool.tile([P, C, R], F32, name="s", bufs=B["s"])
+            q = pool.tile([P, C, R], F32, name="q", bufs=B["q"])
+            nc.scalar.activation(s[:], d["a1"][:].rearrange("p r c -> p c r"), SIGMOID)
+            nc.vector.scalar_tensor_tensor(q[:], s[:], 1.0, d["a3"][:].rearrange("p r c -> p c r"), SUB, MULT)
             gq = quantize("gq", gbf, C, B["gq"])
             w2q = quantize("wq", w2bf, H, B["wq"])
             da1 = pool.tile([P, C, R], BF16, name="da1", bufs=B["da"], align_bytes=64)
             da3 = pool.tile([P, C, R], BF16, name="da3", bufs=B["da"], align_bytes=64)
             half = C // 2
+            ts = []
             for h in range(2):
                 bank = psum.tile([P, R, half], F32, name="dh", bufs=B["dh"])
                 for r in range(R):
                     mm(bank[:, r, :], w2q, r * P, gq, h * half, half, True, True)
                 cols = slice(h * half, (h + 1) * half)
-                if modes[h] == "VV":
-                    turned = bank[:].rearrange("p r c -> p c r")
-                    nc.vector.tensor_tensor(da3[:, cols, :], turned, s[:, :, cols].rearrange("p r c -> p c r"), MULT)
-                    nc.vector.tensor_tensor(da1[:, cols, :], turned, cq[:, :, cols].rearrange("p r c -> p c r"), MULT)
-                    continue
-                t = pool.tile([P, R, half], F32, name="d", bufs=B["d"])
-                if modes[h] == "V":
-                    nc.vector.tensor_tensor(t[:], bank[:], s[:, :, cols], MULT)
-                else:
-                    d0 = pool.tile([P, R, half], F32, name="d0", bufs=B["d0"])
-                    nc.scalar.copy(d0[:], bank[:])
-                    nc.gpsimd.tensor_tensor(t[:], d0[:], s[:, :, cols], MULT)
-                interleave("S", da3[:, cols, :], t[:])
-                nc.gpsimd.tensor_tensor(da1[:, cols, :], t[:].rearrange("p r c -> p c r"), q[:, :, cols].rearrange("p r c -> p c r"), MULT)
+                t = pool.tile([P, half, R], F32, name="d", bufs=B["d"])
+                nc.vector.tensor_tensor(t[:], bank[:].rearrange("p r c -> p c r"), s[:, cols, :], MULT)
+                nc.scalar.copy(da3[:, cols, :], t[:])
+                ts.append((cols, t))
+            for cols, t in ts:
+                nc.vector.scalar_tensor_tensor(da1[:, cols, :], t[:], -1.0, q[:, cols, :], MULT, MULT)
             d["da3q"] = quantize("da3q", da3, C, 2)
             d["da1q"] = quantize("da1q", da1, C, 2)
 
@@ -189,18 +177,18 @@ def tile_moe_bdx_glu_sigmoid_kernel(tc, dyT, a1, a3, w2, w1, w3, gate, offs, out
         gather(2)
         gather(3)
         wall(0)
+        load_a(2)
         load_w(1)
         front(1)
-        load_a(2)
+        front(2)
         wall(1)
         scatter(0)
-        load_w(2)
-        front(2)
         load_a(3)
+        load_w(2)
+        front(3)
         wall(2)
         scatter(1)
         load_w(3)
-        front(3)
         wall(3)
         scatter(2)
         scatter(3)

@@ -14,16 +14,13 @@ FP8X4 = mybir.dt.float8_e4m3fn_x4
 
 P = 128
 R = 4
+HALF = C // 2
+KC = 256
 SIGMOID = mybir.ActivationFunctionType.Sigmoid
 MULT = mybir.AluOpType.mult
-SUB = mybir.AluOpType.subtract
 ADD = mybir.AluOpType.add
-KC = 256
-CHUNKS = K // KC
-W_PLACE = {"0.0.0": "V"}
-A_PLACE = {}
-A_DEF = "VS"
-B = {"x4": 8, "g32": 4, "gbf": 3, "w2raw": 2, "raw": 4, "wbf": 4, "gq": 2, "wq": 8, "s": 2, "u": 1, "q": 2, "da": 2, "d": 4, "d0": 2, "dxs": 6, "dh": 3, "dx": 4}
+SUB = mybir.AluOpType.subtract
+PLACE = ("VVSSSSS", "SSSSSSS")
 
 
 def tile_moe_bdx_glu_sigmoid_kernel(tc, dyT, a1, a3, w2, w1, w3, gate, offs, out):
@@ -36,47 +33,54 @@ def tile_moe_bdx_glu_sigmoid_kernel(tc, dyT, a1, a3, w2, w1, w3, gate, offs, out
         offsets = keep.tile([P, T // 16], U16, name="offsets")
         gates = keep.tile([P, T], F32, name="gates")
         warm = keep.tile([P, 8], F32, name="warm")
-        warm_out = keep.tile([P, 8], F32, name="warm_out")
         windows = [keep.tile([P, T], F32, name="window%d" % b) for b in range(K // P)]
 
         nc.vector.memset(warm[:], 0.0)
-        nc.scalar.activation(warm_out[:], warm[:], SIGMOID)
+        nc.scalar.activation(warm[:], warm[:], SIGMOID)
 
-        dy_view = dyT.rearrange("(p r) c -> p r c", r=R)
         st = [{} for e in range(E)]
+
+        def rows(src):
+            return src.rearrange("(p r) c -> p r c", r=R)
+
+        def slots(e):
+            return slice(e * C, (e + 1) * C)
 
         def offs_of(e):
             return offsets[:, e * (C // 16) : (e + 1) * (C // 16)]
 
-        def load_a(e):
-            t = pool.tile([P, R, H], F32, name="w2raw", bufs=B["w2raw"])
-            nc.sync.dma_start(out=t[:], in_=w2[e].rearrange("(p r) c -> p r c", r=R))
+        def load_first(e):
+            t = pool.tile([P, R, H], F32, name="w2raw", bufs=2)
+            nc.sync.dma_start(out=t[:], in_=rows(w2[e]))
             st[e]["w2"] = t
             for key, src in (("a1", a1), ("a3", a3)):
-                t = pool.tile([P, R, C], F32, name="x4", bufs=B["x4"])
-                nc.sync.dma_start(out=t[:], in_=src.rearrange("(p r) c -> p r c", r=R)[:, :, e * C : (e + 1) * C])
+                t = pool.tile([P, R, C], F32, name="x4", bufs=8)
+                nc.sync.dma_start(out=t[:], in_=rows(src)[:, :, slots(e)])
                 st[e][key] = t
 
-        def load_w(e, split=False):
+        def load_second(e):
             for key in ("w1", "w3"):
-                t = pool.tile([P, R, K], F32, name="w13raw", bufs=B["raw"])
+                t = pool.tile([P, R, K], F32, name="w13raw", bufs=4)
                 st[e][key] = t
-            step = KC if split else K
+            step = KC if e == 0 else K
             for c in range(0, K, step):
                 for key, w in (("w1", w1), ("w3", w3)):
-                    nc.sync.dma_start(out=st[e][key][:, :, c : c + step], in_=w[e].rearrange("(p r) c -> p r c", r=R)[:, :, c : c + step])
+                    nc.sync.dma_start(out=st[e][key][:, :, c : c + step], in_=rows(w[e])[:, :, c : c + step])
 
         def interleave(place, dst, src):
+            out_view = dst.rearrange("p (c i) r -> p c r i", i=2)
+            in_view = src.rearrange("p r (c i) -> p c r i", i=2)
             if place == "G":
-                nc.gpsimd.tensor_scalar(dst, src.rearrange("p r c -> p c r"), 1.0, 0.0, MULT, ADD)
+                nc.gpsimd.tensor_scalar(out_view, in_view, 1.0, 0.0, MULT, ADD)
+            elif place == "V":
+                nc.vector.tensor_copy(out_view, in_view)
             else:
-                copy = nc.vector.tensor_copy if place == "V" else nc.scalar.copy
-                copy(dst.rearrange("p (c i) r -> p c r i", i=4), src.rearrange("p r (c i) -> p c r i", i=4))
+                nc.scalar.copy(out_view, in_view)
 
         def gather(e):
-            t = pool.tile([P, R, C], F32, name="g32", bufs=B["g32"])
+            t = pool.tile([P, R, C], F32, name="g32", bufs=4)
             for r in range(R):
-                nc.vector.tensor_tensor(t[:, r, :], dy[r][:].indirect(offs_of(e)), gates[:, e * C : (e + 1) * C], MULT)
+                nc.vector.tensor_tensor(t[:, r, :], dy[r][:].indirect(offs_of(e)), gates[:, slots(e)], MULT)
             st[e]["g"] = t
 
         def quantize(name, src, words, bufs):
@@ -98,34 +102,31 @@ def tile_moe_bdx_glu_sigmoid_kernel(tc, dyT, a1, a3, w2, w1, w3, gate, offs, out
 
         def front(e):
             d = st[e]
-            gbf = pool.tile([P, C, R], BF16, name="gbf", bufs=B["gbf"], align_bytes=64)
+            place = PLACE[min(e, 1)]
+            gbf = pool.tile([P, C, R], BF16, name="gbf", bufs=3, align_bytes=64)
             interleave("S", gbf[:], d["g"][:])
-            w2bf = pool.tile([P, H, R], BF16, name="wbf", bufs=B["wbf"], align_bytes=64)
-            place = W_PLACE.get("%d.w2" % e, "S")
-            out_view = w2bf[:].rearrange("p (r m) j -> p m j r", r=R)
-            in_view = d["w2"][:].rearrange("p j (m r) -> p m j r", r=R)
-            if place == "G":
-                nc.gpsimd.tensor_scalar(out_view, in_view, 1.0, 0.0, MULT, ADD)
-            elif place == "V":
+            w2bf = pool.tile([P, H, R], BF16, name="wbf", bufs=4, align_bytes=64)
+            out_view = w2bf[:].rearrange("p (r m) j -> p m r j", r=R)
+            in_view = d["w2"][:].rearrange("p j (m r) -> p m r j", r=R)
+            if place[0] == "V":
                 nc.vector.tensor_copy(out_view, in_view)
             else:
                 nc.scalar.copy(out_view, in_view)
-            s = pool.tile([P, C, R], F32, name="s", bufs=B["s"])
-            q = pool.tile([P, C, R], F32, name="q", bufs=B["q"])
-            nc.scalar.activation(s[:], d["a1"][:].rearrange("p r c -> p c r"), SIGMOID)
+            s = pool.tile([P, C, R], F32, name="s", bufs=2)
+            q = pool.tile([P, C, R], F32, name="q", bufs=2)
+            nc.scalar.activation(s[:].rearrange("p (c i) r -> p c r i", i=2), d["a1"][:].rearrange("p r (c i) -> p c r i", i=2), SIGMOID)
             nc.vector.scalar_tensor_tensor(q[:], s[:], 1.0, d["a3"][:].rearrange("p r c -> p c r"), SUB, MULT)
-            gq = quantize("gq", gbf, C, B["gq"])
-            w2q = quantize("wq", w2bf, H, B["wq"])
-            da1 = pool.tile([P, C, R], BF16, name="da1", bufs=B["da"], align_bytes=64)
-            da3 = pool.tile([P, C, R], BF16, name="da3", bufs=B["da"], align_bytes=64)
-            half = C // 2
+            gq = quantize("gq", gbf, C, 2)
+            w2q = quantize("wq", w2bf, H, 8)
+            da1 = pool.tile([P, C, R], BF16, name="da1", bufs=2, align_bytes=64)
+            da3 = pool.tile([P, C, R], BF16, name="da3", bufs=2, align_bytes=64)
             ts = []
             for h in range(2):
-                bank = psum.tile([P, R, half], F32, name="dh", bufs=B["dh"])
+                bank = psum.tile([P, R, HALF], F32, name="dh", bufs=3)
                 for r in range(R):
-                    mm(bank[:, r, :], w2q, r * P, gq, h * half, half, True, True)
-                cols = slice(h * half, (h + 1) * half)
-                t = pool.tile([P, half, R], F32, name="d", bufs=B["d"])
+                    mm(bank[:, r, :], w2q, r * P, gq, h * HALF, HALF, True, True)
+                cols = slice(h * HALF, (h + 1) * HALF)
+                t = pool.tile([P, HALF, R], F32, name="d", bufs=4)
                 nc.vector.tensor_tensor(t[:], bank[:].rearrange("p r c -> p c r"), s[:, cols, :], MULT)
                 nc.scalar.copy(da3[:, cols, :], t[:])
                 ts.append((cols, t))
@@ -134,21 +135,20 @@ def tile_moe_bdx_glu_sigmoid_kernel(tc, dyT, a1, a3, w2, w1, w3, gate, offs, out
             d["da3q"] = quantize("da3q", da3, C, 2)
             d["da1q"] = quantize("da1q", da1, C, 2)
 
-        def wall(e):
+        def multiply(e):
             d = st[e]
+            place = PLACE[min(e, 1)]
             d["dx"] = []
-            for c in range(CHUNKS):
-                wbf = pool.tile([P, 2 * KC, R], BF16, name="wbf", bufs=B["wbf"], align_bytes=64)
+            for c in range(K // KC):
+                wbf = pool.tile([P, 2 * KC, R], BF16, name="wbf", bufs=4, align_bytes=64)
                 for i, key in enumerate(("w1", "w3")):
-                    dst = wbf[:, i * KC : (i + 1) * KC, :]
-                    src = d[key][:, :, c * KC : (c + 1) * KC]
-                    interleave(W_PLACE.get("%d.%d.%d" % (e, c, i), "S"), dst, src)
-                wq = quantize("wq", wbf, 2 * KC, B["wq"])
-                bank = psum.tile([P, 2, C], F32, name="dx", bufs=B["dx"])
+                    interleave(place[1 + 2 * c + i], wbf[:, i * KC : (i + 1) * KC, :], d[key][:, :, c * KC : (c + 1) * KC])
+                wq = quantize("wq", wbf, 2 * KC, 8)
+                bank = psum.tile([P, 2, C], F32, name="dx", bufs=2)
                 for b in range(2):
                     mm(bank[:, b, :], wq, KC + b * P, d["da3q"], 0, C, True, False)
                     mm(bank[:, b, :], wq, b * P, d["da1q"], 0, C, False, True)
-                dx = pool.tile([P, 2, C], F32, name="dxs", bufs=B["dxs"])
+                dx = pool.tile([P, 2, C], F32, name="dxs", bufs=6)
                 nc.scalar.copy(dx[:], bank[:])
                 d["dx"].append(dx)
 
@@ -159,36 +159,22 @@ def tile_moe_bdx_glu_sigmoid_kernel(tc, dyT, a1, a3, w2, w1, w3, gate, offs, out
                     nc.sync.dma_start(out=out[b * P : (b + 1) * P, :], in_=windows[b][:])
 
         nc.sync.dma_start(offsets[:], offs)
-        nc.sync.dma_start(out=gates[:, 0:C], in_=gate[0:P, 0:C])
+        nc.sync.dma_start(out=gates[:, 0 : T // 2], in_=gate[0:P, 0 : T // 2])
         dy = []
         for r in range(R):
-            t = pool.tile([P, T], F32, name="x4", bufs=B["x4"])
+            t = pool.tile([P, T], F32, name="x4", bufs=8)
+            nc.sync.dma_start(out=t[:], in_=rows(dyT)[:, r, :])
             dy.append(t)
-            nc.sync.dma_start(out=t[:], in_=dy_view[:, r, :])
-            if r == 1:
-                nc.sync.dma_start(out=gates[:, C:T], in_=gate[0:P, C:T])
+        nc.sync.dma_start(out=gates[:, T // 2 : T], in_=gate[0:P, T // 2 : T])
 
-        load_a(0)
-        load_w(0, True)
-        load_a(1)
-        gather(0)
-        front(0)
-        gather(1)
-        gather(2)
-        gather(3)
-        wall(0)
-        load_a(2)
-        load_w(1)
-        front(1)
-        front(2)
-        wall(1)
-        scatter(0)
-        load_a(3)
-        load_w(2)
-        front(3)
-        wall(2)
-        scatter(1)
-        load_w(3)
-        wall(3)
-        scatter(2)
-        scatter(3)
+        def stage(work, e):
+            if 0 <= e < E:
+                work(e)
+
+        for step in range(-5, E):
+            stage(gather, step + 5)
+            stage(load_second, step + 2)
+            stage(multiply, step + 1)
+            stage(scatter, step + 0)
+            stage(front, step + 2)
+            stage(load_first, step + 4)

@@ -4,6 +4,7 @@ import concourse.mybir as mybir
 
 K, T, E, C, H, N = 768, 1024, 4, 256, 512, 512
 FLOPS = 2 * T * (N * H + 2 * H * K)
+BYTES = 4 * (N * T + 2 * H * T + E * (N * H + 2 * H * K) + T + K * T) + 2 * 8 * T
 
 F32 = mybir.dt.float32
 BF16 = mybir.dt.bfloat16
@@ -12,15 +13,17 @@ U16 = mybir.dt.uint16
 U8 = mybir.dt.uint8
 FP8X4 = mybir.dt.float8_e4m3fn_x4
 
+SIGMOID = mybir.ActivationFunctionType.Sigmoid
+ADD = mybir.AluOpType.add
+MULT = mybir.AluOpType.mult
+SUBTRACT = mybir.AluOpType.subtract
+
 P = 128
 R = 4
 HALF = C // 2
-KC = 256
-SIGMOID = mybir.ActivationFunctionType.Sigmoid
-MULT = mybir.AluOpType.mult
-ADD = mybir.AluOpType.add
-SUB = mybir.AluOpType.subtract
-PLACE = ("VVSSSSS", "SSSSSSS")
+CHUNK = 256
+CHUNKS = K // CHUNK
+PIECE = 64
 
 
 def tile_moe_bdx_glu_sigmoid_kernel(tc, dyT, a1, a3, w2, w1, w3, gate, offs, out):
@@ -28,7 +31,7 @@ def tile_moe_bdx_glu_sigmoid_kernel(tc, dyT, a1, a3, w2, w1, w3, gate, offs, out
     with ExitStack() as ctx:
         keep = ctx.enter_context(tc.tile_pool(name="keep", bufs=1))
         pool = ctx.enter_context(tc.tile_pool(name="pool", bufs=2))
-        psum = ctx.enter_context(tc.psum_pool(name="psum", bufs=2))
+        psum = ctx.enter_context(tc.psum_pool(name="psum", bufs=1))
 
         offsets = keep.tile([P, T // 16], U16, name="offsets")
         gates = keep.tile([P, T], F32, name="gates")
@@ -38,123 +41,141 @@ def tile_moe_bdx_glu_sigmoid_kernel(tc, dyT, a1, a3, w2, w1, w3, gate, offs, out
         nc.vector.memset(warm[:], 0.0)
         nc.scalar.activation(warm[:], warm[:], SIGMOID)
 
-        st = [{} for e in range(E)]
+        held = [{} for e in range(E)]
 
-        def rows(src):
+        def four_rows(src):
             return src.rearrange("(p r) c -> p r c", r=R)
 
-        def slots(e):
-            return slice(e * C, (e + 1) * C)
+        def offsets_of(first, experts):
+            return offsets[:, first * C // 16 : (first + experts) * C // 16]
 
-        def offs_of(e):
-            return offsets[:, e * (C // 16) : (e + 1) * (C // 16)]
+        def interleave(engine, dst, src):
+            if engine is nc.gpsimd:
+                nc.gpsimd.tensor_scalar(dst, src.rearrange("p r c -> p c r"), 1.0, 0.0, MULT, ADD)
+                return
+            copy = nc.vector.tensor_copy if engine is nc.vector else nc.scalar.copy
+            copy(dst.rearrange("p (c i) r -> p c r i", i=2), src.rearrange("p r (c i) -> p c r i", i=2))
 
-        def load_first(e):
-            t = pool.tile([P, R, H], F32, name="w2raw", bufs=2)
-            nc.sync.dma_start(out=t[:], in_=rows(w2[e]))
-            st[e]["w2"] = t
-            for key, src in (("a1", a1), ("a3", a3)):
-                t = pool.tile([P, R, C], F32, name="x4", bufs=8)
-                nc.sync.dma_start(out=t[:], in_=rows(src)[:, :, slots(e)])
-                st[e][key] = t
-
-        def load_second(e):
-            for key in ("w1", "w3"):
-                t = pool.tile([P, R, K], F32, name="w13raw", bufs=4)
-                st[e][key] = t
-            step = KC if e == 0 else K
-            for c in range(0, K, step):
-                for key, w in (("w1", w1), ("w3", w3)):
-                    nc.sync.dma_start(out=st[e][key][:, :, c : c + step], in_=rows(w[e])[:, :, c : c + step])
-
-        def interleave(place, dst, src):
-            out_view = dst.rearrange("p (c i) r -> p c r i", i=2)
-            in_view = src.rearrange("p r (c i) -> p c r i", i=2)
-            if place == "G":
-                nc.gpsimd.tensor_scalar(out_view, in_view, 1.0, 0.0, MULT, ADD)
-            elif place == "V":
-                nc.vector.tensor_copy(out_view, in_view)
-            else:
-                nc.scalar.copy(out_view, in_view)
-
-        def gather(e):
-            t = pool.tile([P, R, C], F32, name="g32", bufs=4)
-            for r in range(R):
-                nc.vector.tensor_tensor(t[:, r, :], dy[r][:].indirect(offs_of(e)), gates[:, slots(e)], MULT)
-            st[e]["g"] = t
-
-        def quantize(name, src, words, bufs):
-            codes = pool.tile([P, words], U32, name=name, bufs=bufs, align_bytes=64)
-            scales = pool.tile([P, words], U8, name=name + "_s", bufs=bufs, align_bytes=64)
+        def quantize(name, src, bufs):
+            columns = src.shape[1]
+            codes = pool.tile([P, columns], U32, name=name, bufs=bufs, align_bytes=64)
+            scales = pool.tile([P, columns], U8, name=name + "_scales", bufs=bufs, align_bytes=64)
             nc.vector.quantize_mx(out=codes[:].bitcast(FP8X4), scales=scales[:], in_=src[:].rearrange("p c r -> p (c r)"))
             return codes, scales
 
-        def mm(bank, lhs, l0, rhs, r0, n, start, stop):
+        def multiply_mx(bank, stationary, s0, moving, m0, columns, start, stop):
             nc.tensor.matmul_mx(
                 out=bank,
-                lhsT=lhs[0][:, l0 : l0 + P].bitcast(FP8X4),
-                lhsT_scale=lhs[1][:, l0 : l0 + P],
-                rhs=rhs[0][:, r0 : r0 + n].bitcast(FP8X4),
-                rhs_scale=rhs[1][:, r0 : r0 + n],
+                lhsT=stationary[0][:, s0 : s0 + P].bitcast(FP8X4),
+                lhsT_scale=stationary[1][:, s0 : s0 + P],
+                rhs=moving[0][:, m0 : m0 + columns].bitcast(FP8X4),
+                rhs_scale=moving[1][:, m0 : m0 + columns],
                 start=start,
                 stop=stop,
             )
 
-        def front(e):
-            d = st[e]
-            place = PLACE[min(e, 1)]
-            gbf = pool.tile([P, C, R], BF16, name="gbf", bufs=3, align_bytes=64)
-            interleave("S", gbf[:], d["g"][:])
-            w2bf = pool.tile([P, H, R], BF16, name="wbf", bufs=4, align_bytes=64)
-            out_view = w2bf[:].rearrange("p (r m) j -> p m r j", r=R)
-            in_view = d["w2"][:].rearrange("p j (m r) -> p m r j", r=R)
-            if place[0] == "V":
-                nc.vector.tensor_copy(out_view, in_view)
-            else:
-                nc.scalar.copy(out_view, in_view)
+        def load_first(e):
+            h = held[e]
+            h["w2"] = pool.tile([P, R, H], F32, name="w2_raw", bufs=2)
+            nc.sync.dma_start(out=h["w2"][:], in_=four_rows(w2[e]))
+            for key, src in (("a1", a1), ("a3", a3)):
+                h[key] = pool.tile([P, R, C], F32, name="rows_4k", bufs=8)
+                nc.sync.dma_start(out=h[key][:], in_=four_rows(src)[:, :, e * C : (e + 1) * C])
+
+        def load_second(e):
+            h = held[e]
+            for key in ("w1", "w3"):
+                h[key] = pool.tile([P, R, K], F32, name="w13_raw", bufs=4)
+            step = CHUNK if e == 0 else K
+            for k0 in range(0, K, step):
+                for key, src in (("w1", w1), ("w3", w3)):
+                    nc.sync.dma_start(out=h[key][:, :, k0 : k0 + step], in_=four_rows(src[e])[:, :, k0 : k0 + step])
+
+        def gather(e):
+            if e % 2 == 1:
+                return
+            g = pool.tile([P, R, 2 * C], F32, name="g", bufs=2)
+            for r in range(R):
+                nc.vector.tensor_tensor(g[:, r, :], dy[r][:].indirect(offsets_of(e, 2)), gates[:, e * C : (e + 2) * C], MULT)
+            held[e]["g"] = g[:, :, 0:C]
+            held[e + 1]["g"] = g[:, :, C : 2 * C]
+
+        def first_product(e):
+            h = held[e]
+            g_bf = pool.tile([P, C, R], BF16, name="g_bf", bufs=3, align_bytes=64)
+            interleave(nc.scalar, g_bf[:], h["g"])
+
+            w2_bf = pool.tile([P, H, R], BF16, name="w_bf", bufs=3, align_bytes=64)
+            nc.scalar.copy(
+                w2_bf[:].rearrange("p (r m) j -> p m r j", r=R),
+                h["w2"][:].rearrange("p j (m r) -> p m r j", r=R),
+            )
+
             s = pool.tile([P, C, R], F32, name="s", bufs=2)
             q = pool.tile([P, C, R], F32, name="q", bufs=2)
-            nc.scalar.activation(s[:].rearrange("p (c i) r -> p c r i", i=2), d["a1"][:].rearrange("p r (c i) -> p c r i", i=2), SIGMOID)
-            nc.vector.scalar_tensor_tensor(q[:], s[:], 1.0, d["a3"][:].rearrange("p r c -> p c r"), SUB, MULT)
-            gq = quantize("gq", gbf, C, 2)
-            w2q = quantize("wq", w2bf, H, 8)
-            da1 = pool.tile([P, C, R], BF16, name="da1", bufs=2, align_bytes=64)
-            da3 = pool.tile([P, C, R], BF16, name="da3", bufs=2, align_bytes=64)
-            ts = []
-            for h in range(2):
-                bank = psum.tile([P, R, HALF], F32, name="dh", bufs=3)
-                for r in range(R):
-                    mm(bank[:, r, :], w2q, r * P, gq, h * HALF, HALF, True, True)
-                cols = slice(h * HALF, (h + 1) * HALF)
-                t = pool.tile([P, HALF, R], F32, name="d", bufs=4)
-                nc.vector.tensor_tensor(t[:], bank[:].rearrange("p r c -> p c r"), s[:, cols, :], MULT)
-                nc.scalar.copy(da3[:, cols, :], t[:])
-                ts.append((cols, t))
-            for cols, t in ts:
-                nc.vector.scalar_tensor_tensor(da1[:, cols, :], t[:], -1.0, q[:, cols, :], MULT, MULT)
-            d["da3q"] = quantize("da3q", da3, C, 2)
-            d["da1q"] = quantize("da1q", da1, C, 2)
+            pairs_a1 = h["a1"][:].rearrange("p r (c i) -> p c r i", i=2)
+            turned_a3 = h["a3"][:].rearrange("p r c -> p c r")
+            nc.scalar.activation(s[:].rearrange("p (c i) r -> p c r i", i=2), pairs_a1, SIGMOID)
+            on_gpsimd = e >= E // 2
+            if on_gpsimd:
+                u = pool.tile([P, C, R], F32, name="u", bufs=1)
+                nc.scalar.activation(u[:].rearrange("p (c i) r -> p c r i", i=2), pairs_a1, SIGMOID, scale=-1.0)
+                for c0 in range(0, C, PIECE):
+                    cols = slice(c0, c0 + PIECE)
+                    nc.gpsimd.tensor_tensor(q[:, cols, :], turned_a3[:, cols, :], u[:, cols, :], MULT)
+            else:
+                nc.vector.scalar_tensor_tensor(q[:], s[:], 1.0, turned_a3, SUBTRACT, MULT)
 
-        def multiply(e):
-            d = st[e]
-            place = PLACE[min(e, 1)]
-            d["dx"] = []
-            for c in range(K // KC):
-                wbf = pool.tile([P, 2 * KC, R], BF16, name="wbf", bufs=4, align_bytes=64)
+            gq = quantize("gq", g_bf, 2)
+            w2q = quantize("wq", w2_bf, 8)
+
+            da = pool.tile([P, 2 * C, R], BF16, name="da", bufs=1, align_bytes=64)
+            da3 = pool.tile([P, C, R], F32, name="da3", bufs=2)
+            for c0 in range(0, C, HALF):
+                bank = psum.tile([P, R, HALF], F32, name="dh", bufs=1)
+                for r in range(R):
+                    multiply_mx(bank[:, r, :], w2q, r * P, gq, c0, HALF, True, True)
+                cols = slice(c0, c0 + HALF)
+                nc.vector.tensor_tensor(da3[:, cols, :], bank[:].rearrange("p r c -> p c r"), s[:, cols, :], MULT)
+                nc.scalar.copy(da[:, C + c0 : C + c0 + HALF, :], da3[:, cols, :])
+                if on_gpsimd:
+                    nc.gpsimd.tensor_tensor(da[:, cols, :], da3[:, cols, :], q[:, cols, :], MULT)
+            if not on_gpsimd:
+                nc.vector.scalar_tensor_tensor(da[:, 0:C, :], da3[:], -1.0, q[:], MULT, MULT)
+            h["daq"] = quantize("daq", da, 3)
+
+        def copy_engine(e, c, key):
+            if key == "w1" and (e == 0 or c == CHUNKS - 1):
+                return nc.gpsimd
+            if key == "w3" and e == 0 and c == 0:
+                return nc.vector
+            return nc.scalar
+
+        def prepare_second(e):
+            h = held[e]
+            h["wq"] = []
+            for c in range(CHUNKS):
+                w_bf = pool.tile([P, 2 * CHUNK, R], BF16, name="w_bf", bufs=3, align_bytes=64)
                 for i, key in enumerate(("w1", "w3")):
-                    interleave(place[1 + 2 * c + i], wbf[:, i * KC : (i + 1) * KC, :], d[key][:, :, c * KC : (c + 1) * KC])
-                wq = quantize("wq", wbf, 2 * KC, 8)
-                bank = psum.tile([P, 2, C], F32, name="dx", bufs=2)
-                for b in range(2):
-                    mm(bank[:, b, :], wq, KC + b * P, d["da3q"], 0, C, True, False)
-                    mm(bank[:, b, :], wq, b * P, d["da1q"], 0, C, False, True)
-                dx = pool.tile([P, 2, C], F32, name="dxs", bufs=6)
+                    interleave(copy_engine(e, c, key), w_bf[:, i * CHUNK : (i + 1) * CHUNK, :], h[key][:, :, c * CHUNK : (c + 1) * CHUNK])
+                h["wq"].append(quantize("wq", w_bf, 8))
+
+        def second_product(e):
+            h = held[e]
+            h["dx"] = []
+            for b in range(K // P):
+                wq = h["wq"][b * P // CHUNK]
+                k0 = b * P % CHUNK
+                bank = psum.tile([P, C], F32, name="dx_bank", bufs=1)
+                multiply_mx(bank[:], wq, CHUNK + k0, h["daq"], C, C, True, False)
+                multiply_mx(bank[:], wq, k0, h["daq"], 0, C, False, True)
+                dx = pool.tile([P, C], F32, name="dx", bufs=8)
                 nc.scalar.copy(dx[:], bank[:])
-                d["dx"].append(dx)
+                h["dx"].append(dx)
 
         def scatter(e):
             for b in range(K // P):
-                nc.vector.tensor_copy(windows[b][:].indirect(offs_of(e)), st[e]["dx"][b // 2][:, b % 2, :])
+                nc.vector.tensor_copy(windows[b][:].indirect(offsets_of(e, 1)), held[e]["dx"][b][:])
                 if e == E - 1:
                     nc.sync.dma_start(out=out[b * P : (b + 1) * P, :], in_=windows[b][:])
 
@@ -162,19 +183,21 @@ def tile_moe_bdx_glu_sigmoid_kernel(tc, dyT, a1, a3, w2, w1, w3, gate, offs, out
         nc.sync.dma_start(out=gates[:, 0 : T // 2], in_=gate[0:P, 0 : T // 2])
         dy = []
         for r in range(R):
-            t = pool.tile([P, T], F32, name="x4", bufs=8)
-            nc.sync.dma_start(out=t[:], in_=rows(dyT)[:, r, :])
-            dy.append(t)
+            rows = pool.tile([P, T], F32, name="rows_4k", bufs=8)
+            nc.sync.dma_start(out=rows[:], in_=four_rows(dyT)[:, r, :])
+            dy.append(rows)
         nc.sync.dma_start(out=gates[:, T // 2 : T], in_=gate[0:P, T // 2 : T])
 
-        def stage(work, e):
-            if 0 <= e < E:
-                work(e)
-
-        for step in range(-5, E):
-            stage(gather, step + 5)
-            stage(load_second, step + 2)
-            stage(multiply, step + 1)
-            stage(scatter, step + 0)
-            stage(front, step + 2)
-            stage(load_first, step + 4)
+        stages = (
+            (scatter, 0),
+            (gather, 4),
+            (load_first, 3),
+            (prepare_second, 1),
+            (second_product, 1),
+            (load_second, 2),
+            (first_product, 3),
+        )
+        for t in range(-4, E):
+            for stage, ahead in stages:
+                if 0 <= t + ahead < E:
+                    stage(t + ahead)

from contextlib import ExitStack

import concourse.mybir as mybir

K, T, E, C, H, N = 768, 1024, 4, 256, 512, 512
FLOPS = 2 * T * (N * H + 2 * H * K)
BYTES = 4 * (N * T + 2 * H * T + E * (N * H + 2 * H * K) + T + K * T) + 2 * 8 * T

F32 = mybir.dt.float32
BF16 = mybir.dt.bfloat16
U32 = mybir.dt.uint32
U16 = mybir.dt.uint16
U8 = mybir.dt.uint8
FP8X4 = mybir.dt.float8_e4m3fn_x4

SIGMOID = mybir.ActivationFunctionType.Sigmoid
ADD = mybir.AluOpType.add
MULT = mybir.AluOpType.mult
SUBTRACT = mybir.AluOpType.subtract

P = 128
R = 4
HALF = C // 2
CHUNK = 256
CHUNKS = K // CHUNK
PIECE = 64


def tile_moe_bdx_glu_sigmoid_kernel(tc, dyT, a1, a3, w2, w1, w3, gate, offs, out):
    nc = tc.nc
    with ExitStack() as ctx:
        keep = ctx.enter_context(tc.tile_pool(name="keep", bufs=1))
        pool = ctx.enter_context(tc.tile_pool(name="pool", bufs=2))
        psum = ctx.enter_context(tc.psum_pool(name="psum", bufs=1))

        offsets = keep.tile([P, T // 16], U16, name="offsets")
        gates = keep.tile([P, T], F32, name="gates")
        warm = keep.tile([P, 8], F32, name="warm")
        windows = [keep.tile([P, T], F32, name="window%d" % b) for b in range(K // P)]

        nc.vector.memset(warm[:], 0.0)
        nc.scalar.activation(warm[:], warm[:], SIGMOID)

        held = [{} for e in range(E)]

        def four_rows(src):
            return src.rearrange("(p r) c -> p r c", r=R)

        def offsets_of(first, experts):
            return offsets[:, first * C // 16 : (first + experts) * C // 16]

        def interleave(engine, dst, src):
            if engine is nc.gpsimd:
                nc.gpsimd.tensor_scalar(dst, src.rearrange("p r c -> p c r"), 1.0, 0.0, MULT, ADD)
                return
            copy = nc.vector.tensor_copy if engine is nc.vector else nc.scalar.copy
            copy(dst.rearrange("p (c i) r -> p c r i", i=2), src.rearrange("p r (c i) -> p c r i", i=2))

        def quantize(name, src, bufs):
            columns = src.shape[1]
            codes = pool.tile([P, columns], U32, name=name, bufs=bufs, align_bytes=64)
            scales = pool.tile([P, columns], U8, name=name + "_scales", bufs=bufs, align_bytes=64)
            nc.vector.quantize_mx(out=codes[:].bitcast(FP8X4), scales=scales[:], in_=src[:].rearrange("p c r -> p (c r)"))
            return codes, scales

        def multiply_mx(bank, stationary, s0, moving, m0, columns, start, stop):
            nc.tensor.matmul_mx(
                out=bank,
                lhsT=stationary[0][:, s0 : s0 + P].bitcast(FP8X4),
                lhsT_scale=stationary[1][:, s0 : s0 + P],
                rhs=moving[0][:, m0 : m0 + columns].bitcast(FP8X4),
                rhs_scale=moving[1][:, m0 : m0 + columns],
                start=start,
                stop=stop,
            )

        def load_first(e):
            h = held[e]
            h["w2"] = pool.tile([P, R, H], F32, name="w2_raw", bufs=2)
            nc.sync.dma_start(out=h["w2"][:], in_=four_rows(w2[e]))
            for key, src in (("a1", a1), ("a3", a3)):
                h[key] = pool.tile([P, R, C], F32, name="rows_4k", bufs=8)
                nc.sync.dma_start(out=h[key][:], in_=four_rows(src)[:, :, e * C : (e + 1) * C])

        def load_second(e):
            h = held[e]
            for key in ("w1", "w3"):
                h[key] = pool.tile([P, R, K], F32, name="w13_raw", bufs=4)
            step = CHUNK if e == 0 else K
            for k0 in range(0, K, step):
                for key, src in (("w1", w1), ("w3", w3)):
                    nc.sync.dma_start(out=h[key][:, :, k0 : k0 + step], in_=four_rows(src[e])[:, :, k0 : k0 + step])

        def gather(e):
            if e % 2 == 1:
                return
            g = pool.tile([P, R, 2 * C], F32, name="g", bufs=2)
            for r in range(R):
                nc.vector.tensor_tensor(g[:, r, :], dy[r][:].indirect(offsets_of(e, 2)), gates[:, e * C : (e + 2) * C], MULT)
            held[e]["g"] = g[:, :, 0:C]
            held[e + 1]["g"] = g[:, :, C : 2 * C]

        def first_product(e):
            h = held[e]
            g_bf = pool.tile([P, C, R], BF16, name="g_bf", bufs=3, align_bytes=64)
            interleave(nc.scalar, g_bf[:], h["g"])

            w2_bf = pool.tile([P, H, R], BF16, name="w_bf", bufs=3, align_bytes=64)
            nc.scalar.copy(
                w2_bf[:].rearrange("p (r m) j -> p m r j", r=R),
                h["w2"][:].rearrange("p j (m r) -> p m r j", r=R),
            )

            s = pool.tile([P, C, R], F32, name="s", bufs=2)
            q = pool.tile([P, C, R], F32, name="q", bufs=2)
            pairs_a1 = h["a1"][:].rearrange("p r (c i) -> p c r i", i=2)
            turned_a3 = h["a3"][:].rearrange("p r c -> p c r")
            nc.scalar.activation(s[:].rearrange("p (c i) r -> p c r i", i=2), pairs_a1, SIGMOID)
            on_gpsimd = e >= E // 2
            if on_gpsimd:
                u = pool.tile([P, C, R], F32, name="u", bufs=1)
                nc.scalar.activation(u[:].rearrange("p (c i) r -> p c r i", i=2), pairs_a1, SIGMOID, scale=-1.0)
                for c0 in range(0, C, PIECE):
                    cols = slice(c0, c0 + PIECE)
                    nc.gpsimd.tensor_tensor(q[:, cols, :], turned_a3[:, cols, :], u[:, cols, :], MULT)
            else:
                nc.vector.scalar_tensor_tensor(q[:], s[:], 1.0, turned_a3, SUBTRACT, MULT)

            gq = quantize("gq", g_bf, 2)
            w2q = quantize("wq", w2_bf, 8)

            da = pool.tile([P, 2 * C, R], BF16, name="da", bufs=1, align_bytes=64)
            da3 = pool.tile([P, C, R], F32, name="da3", bufs=2)
            for c0 in range(0, C, HALF):
                bank = psum.tile([P, R, HALF], F32, name="dh", bufs=1)
                for r in range(R):
                    multiply_mx(bank[:, r, :], w2q, r * P, gq, c0, HALF, True, True)
                cols = slice(c0, c0 + HALF)
                nc.vector.tensor_tensor(da3[:, cols, :], bank[:].rearrange("p r c -> p c r"), s[:, cols, :], MULT)
                nc.scalar.copy(da[:, C + c0 : C + c0 + HALF, :], da3[:, cols, :])
                if on_gpsimd:
                    nc.gpsimd.tensor_tensor(da[:, cols, :], da3[:, cols, :], q[:, cols, :], MULT)
            if not on_gpsimd:
                nc.vector.scalar_tensor_tensor(da[:, 0:C, :], da3[:], -1.0, q[:], MULT, MULT)
            h["daq"] = quantize("daq", da, 3)

        def copy_engine(e, c, key):
            if key == "w1" and (e == 0 or c == CHUNKS - 1):
                return nc.gpsimd
            if key == "w3" and e == 0 and c == 0:
                return nc.vector
            return nc.scalar

        def prepare_second(e):
            h = held[e]
            h["wq"] = []
            for c in range(CHUNKS):
                w_bf = pool.tile([P, 2 * CHUNK, R], BF16, name="w_bf", bufs=3, align_bytes=64)
                for i, key in enumerate(("w1", "w3")):
                    interleave(copy_engine(e, c, key), w_bf[:, i * CHUNK : (i + 1) * CHUNK, :], h[key][:, :, c * CHUNK : (c + 1) * CHUNK])
                h["wq"].append(quantize("wq", w_bf, 8))

        def second_product(e):
            h = held[e]
            h["dx"] = []
            for b in range(K // P):
                wq = h["wq"][b * P // CHUNK]
                k0 = b * P % CHUNK
                bank = psum.tile([P, C], F32, name="dx_bank", bufs=1)
                multiply_mx(bank[:], wq, CHUNK + k0, h["daq"], C, C, True, False)
                multiply_mx(bank[:], wq, k0, h["daq"], 0, C, False, True)
                dx = pool.tile([P, C], F32, name="dx", bufs=8)
                nc.scalar.copy(dx[:], bank[:])
                h["dx"].append(dx)

        def scatter(e):
            for b in range(K // P):
                nc.vector.tensor_copy(windows[b][:].indirect(offsets_of(e, 1)), held[e]["dx"][b][:])
                if e == E - 1:
                    nc.sync.dma_start(out=out[b * P : (b + 1) * P, :], in_=windows[b][:])

        nc.sync.dma_start(offsets[:], offs)
        nc.sync.dma_start(out=gates[:, 0 : T // 2], in_=gate[0:P, 0 : T // 2])
        dy = []
        for r in range(R):
            rows = pool.tile([P, T], F32, name="rows_4k", bufs=8)
            nc.sync.dma_start(out=rows[:], in_=four_rows(dyT)[:, r, :])
            dy.append(rows)
        nc.sync.dma_start(out=gates[:, T // 2 : T], in_=gate[0:P, T // 2 : T])

        stages = (
            (scatter, 0),
            (gather, 4),
            (load_first, 3),
            (prepare_second, 1),
            (second_product, 1),
            (load_second, 2),
            (first_product, 3),
        )
        for t in range(-4, E):
            for stage, ahead in stages:
                if 0 <= t + ahead < E:
                    stage(t + ahead)
